import numpy as np
import ml_dtypes


def mxq(x, axis, fmt="e4m3"):
    dtype, down = {"e4m3": (ml_dtypes.float8_e4m3fn, 7), "e5m2": (ml_dtypes.float8_e5m2, 14)}[fmt]
    v = np.moveaxis(np.asarray(x, np.float32).astype(ml_dtypes.bfloat16).astype(np.float64), axis, -1)
    blocks = v.reshape(v.shape[:-1] + (-1, 32))
    amax = np.abs(blocks).max(-1, keepdims=True)
    byte = np.maximum(np.where(amax > 0, np.frexp(amax)[1] - 1 + 127, 0) - down, 1)
    scale = np.exp2(byte - 127.0)
    codes = (blocks / scale).astype(np.float32).astype(dtype).astype(np.float64)
    return np.moveaxis((codes * scale).reshape(v.shape), -1, axis)


WIDE = False


def mx_kscale(k):
    if not WIDE:
        return np.ones(k)
    levels = np.array([10, -10, 5, -5, 0])
    if k % 512:
        return np.exp2(np.random.permutation(np.resize(levels, k // 32))).repeat(32)
    a = np.empty((k // 512, 16))
    for p in range(k // 512):
        a[p, :8] = np.random.permutation(np.resize(levels, 8))
        for g in range(8):
            far = levels[np.abs(levels - a[p, g]) >= 10]
            a[p, g + 8] = far[np.random.randint(len(far))]
    return np.exp2(a.ravel()).repeat(32)


def f64(x):
    return np.asarray(x).astype(np.float64)


def striped(idx):
    return np.tile(np.asarray(idx).reshape(-1, 16).T, (8, 1)).astype(np.uint16)


def unstriped(offs):
    return offs[:16].T.reshape(-1).astype(np.int64)


B, N, T, D, DV, NQ = 1, 512, 1024, 512, 0, 128


def setup_inputs():
    n = np.random.standard_normal
    idx = np.random.permutation(T)[:B * N]
    s = mx_kscale(D)[:, None]
    return {
        "qT": (n((B, D, NQ)) * s * (1.00 / np.sqrt(D))).astype(np.float32),
        "kT": (n((D, T)) / s).astype(np.float32),
        "offs": striped(idx),
    }


def reference(qT, kT, offs):
    idx = unstriped(offs)
    pick = lambda x: x[:, idx].reshape(x.shape[0], B, N).transpose(1, 0, 2)
    a = mxq(f64(qT), 1, "e4m3").transpose(0, 2, 1) @ mxq(pick(f64(kT)), 1, "e4m3")
    out = np.zeros((B, NQ, T))
    for b in range(B):
        out[b][:, idx[b * N:(b + 1) * N]] = a[b]
    return out

@@ -1,0 +1,104 @@
+from contextlib import ExitStack
+
+import concourse.mybir as mybir
+
+N, T, D, NQ = 512, 1024, 512, 128
+P = 128
+PACK = 4
+FLOPS = 2 * NQ * D * N
+
+F32 = mybir.dt.float32
+BF16 = mybir.dt.bfloat16
+U32 = mybir.dt.uint32
+U16 = mybir.dt.uint16
+U8 = mybir.dt.uint8
+FP8X4 = mybir.dt.float8_e4m3fn_x4
+
+CHUNKS = ((0, 128), (128, 256), (256, 512))
+
+
+def tile_attend_sddmm_kernel(tc, qT, kT, offs, out):
+    nc = tc.nc
+    k_rows = kT.rearrange("(p j) t -> j p t", j=PACK)
+    q_rows = qT[0].rearrange("(p j) q -> p j q", j=PACK)
+
+    with ExitStack() as ctx:
+        keep = ctx.enter_context(tc.tile_pool(name="keep", bufs=1))
+        psum = ctx.enter_context(tc.psum_pool(name="psum", bufs=1))
+
+        offsets = keep.tile([P, N // 16], U16, name="offsets")
+        planes = [keep.tile([P, T], F32, name=f"plane{j}") for j in range(PACK)]
+        q_raw = keep.tile([P, PACK, NQ], F32, name="q_raw")
+
+        nc.sync.dma_start(offsets[:], offs)
+        nc.sync.dma_start(planes[0][:], k_rows[0])
+        nc.sync.dma_start(planes[1][:], k_rows[1])
+        nc.sync.dma_start(planes[2][:], k_rows[2])
+        nc.sync.dma_start(q_raw[:], q_rows)
+        nc.sync.dma_start(planes[3][:], k_rows[3])
+
+        window = keep.tile([P, T], F32, name="window")
+        nc.vector.memset(window[:], 0.0)
+
+        picked = keep.tile([P, 2, N], F32, name="picked")
+        keys = keep.tile([P, N, PACK], BF16, align_bytes=64, name="keys")
+        q_grouped = keep.tile([P, NQ, PACK], BF16, align_bytes=64, name="q_grouped")
+        q_codes = keep.tile([P, NQ], U32, align_bytes=64, name="q_codes")
+        q_scales = keep.tile([P, NQ], U8, align_bytes=64, name="q_scales")
+
+        nc.vector.tensor_copy(picked[:, 0, :], planes[0][:].indirect(offsets[:]))
+        nc.vector.tensor_copy(picked[:, 1, :], planes[1][:].indirect(offsets[:]))
+        nc.scalar.copy(keys[:, :, 0:2], picked[:].rearrange("p t n -> p n t"))
+        nc.vector.tensor_copy(keys[:, :, 2], planes[2][:].indirect(offsets[:]))
+        nc.scalar.copy(q_grouped[:], q_raw[:].rearrange("p j q -> p q j"))
+        nc.vector.quantize_mx(
+            out=q_codes[:].bitcast(FP8X4),
+            scales=q_scales[:],
+            in_=q_grouped[:].rearrange("p q j -> p (q j)"),
+        )
+
+        codes = []
+        scales = []
+        results = []
+        for c, (lo, hi) in enumerate(CHUNKS):
+            codes.append(keep.tile([P, hi - lo], U32, align_bytes=64, name=f"codes{c}"))
+            scales.append(keep.tile([P, hi - lo], U8, align_bytes=64, name=f"scales{c}"))
+            results.append(keep.tile([P, hi - lo], F32, name=f"result{c}"))
+
+        def gather(c):
+            lo, hi = CHUNKS[c]
+            nc.vector.tensor_copy(keys[:, lo:hi, 3], planes[3][:].indirect(offsets[:, lo // 16 : hi // 16]))
+
+        def multiply(c):
+            lo, hi = CHUNKS[c]
+            nc.vector.quantize_mx(
+                out=codes[c][:].bitcast(FP8X4),
+                scales=scales[c][:],
+                in_=keys[:, lo:hi, :].rearrange("p n j -> p (n j)"),
+            )
+            acc = psum.tile([NQ, hi - lo], F32, name=f"acc{c}")
+            nc.tensor.matmul_mx(
+                out=acc[:],
+                lhsT=q_codes[:].bitcast(FP8X4),
+                lhsT_scale=q_scales[:],
+                rhs=codes[c][:].bitcast(FP8X4),
+                rhs_scale=scales[c][:],
+                start=True,
+                stop=True,
+            )
+            nc.scalar.copy(results[c][:], acc[:])
+
+        def scatter(c):
+            lo, hi = CHUNKS[c]
+            nc.vector.tensor_copy(window[:].indirect(offsets[:, lo // 16 : hi // 16]), results[c][:])
+
+        gather(0)
+        gather(1)
+        multiply(0)
+        gather(2)
+        multiply(1)
+        scatter(0)
+        multiply(2)
+        scatter(1)
+        scatter(2)
+        nc.sync.dma_start(out[0], window[:])

@@ -12,6 +12,7 @@ BF16 = mybir.dt.bfloat16
 U32 = mybir.dt.uint32
 U16 = mybir.dt.uint16
 U8 = mybir.dt.uint8
+COPY = mybir.ActivationFunctionType.Copy
 FP8X4 = mybir.dt.float8_e4m3fn_x4
 
 CHUNKS = ((0, 128), (128, 256), (256, 512))
@@ -34,48 +35,56 @@ def tile_attend_sddmm_kernel(tc, qT, kT, offs, out):
         nc.sync.dma_start(planes[0][:], k_rows[0])
         nc.sync.dma_start(planes[1][:], k_rows[1])
         nc.sync.dma_start(planes[2][:], k_rows[2])
-        nc.sync.dma_start(q_raw[:], q_rows)
         nc.sync.dma_start(planes[3][:], k_rows[3])
+        nc.sync.dma_start(q_raw[:], q_rows)
 
         window = keep.tile([P, T], F32, name="window")
         nc.vector.memset(window[:], 0.0)
 
-        picked = keep.tile([P, 2, N], F32, name="picked")
+        warm = keep.tile([P, 8], F32, name="warm")
+        warmed = keep.tile([P, 8], F32, name="warmed")
+        nc.vector.memset(warm[:], 0.0)
+        nc.scalar.activation(warmed[:], warm[:], COPY)
+
+        rounded = [keep.tile([P, T], BF16, name=f"rounded{j}") for j in range(PACK)]
         keys = keep.tile([P, N, PACK], BF16, align_bytes=64, name="keys")
         q_grouped = keep.tile([P, NQ, PACK], BF16, align_bytes=64, name="q_grouped")
         q_codes = keep.tile([P, NQ], U32, align_bytes=64, name="q_codes")
         q_scales = keep.tile([P, NQ], U8, align_bytes=64, name="q_scales")
 
-        nc.vector.tensor_copy(picked[:, 0, :], planes[0][:].indirect(offsets[:]))
-        nc.vector.tensor_copy(picked[:, 1, :], planes[1][:].indirect(offsets[:]))
-        nc.scalar.copy(keys[:, :, 0:2], picked[:].rearrange("p t n -> p n t"))
-        nc.vector.tensor_copy(keys[:, :, 2], planes[2][:].indirect(offsets[:]))
-        nc.scalar.copy(q_grouped[:], q_raw[:].rearrange("p j q -> p q j"))
-        nc.vector.quantize_mx(
-            out=q_codes[:].bitcast(FP8X4),
-            scales=q_scales[:],
-            in_=q_grouped[:].rearrange("p q j -> p (q j)"),
-        )
+        def on_vector(j, lo, hi):
+            nc.vector.tensor_copy(keys[:, lo:hi, j], planes[j][:].indirect(offsets[:, lo // 16 : hi // 16]))
+
+        def on_scalar(j, lo, hi):
+            nc.scalar.activation(keys[:, lo:hi, j], rounded[j][:].indirect(offsets[:, lo // 16 : hi // 16]), COPY)
+
+        for j in (0, 1):
+            nc.vector.tensor_copy(rounded[j][:], planes[j][:])
+            on_scalar(j, 0, 256)
+            on_vector(j, 256, 512)
+        nc.scalar.activation(rounded[2][:], planes[2][:], COPY)
+        on_scalar(2, 256, 512)
+        on_vector(2, 0, 256)
+        nc.vector.tensor_copy(rounded[3][:], planes[3][:])
+        on_scalar(3, 256, 512)
 
         codes = []
         scales = []
-        results = []
+        result = keep.tile([NQ, N], F32, name="result")
         for c, (lo, hi) in enumerate(CHUNKS):
             codes.append(keep.tile([P, hi - lo], U32, align_bytes=64, name=f"codes{c}"))
             scales.append(keep.tile([P, hi - lo], U8, align_bytes=64, name=f"scales{c}"))
-            results.append(keep.tile([P, hi - lo], F32, name=f"result{c}"))
 
-        def gather(c):
-            lo, hi = CHUNKS[c]
-            nc.vector.tensor_copy(keys[:, lo:hi, 3], planes[3][:].indirect(offsets[:, lo // 16 : hi // 16]))
-
-        def multiply(c):
+        def quantise(c):
             lo, hi = CHUNKS[c]
             nc.vector.quantize_mx(
                 out=codes[c][:].bitcast(FP8X4),
                 scales=scales[c][:],
                 in_=keys[:, lo:hi, :].rearrange("p n j -> p (n j)"),
             )
+
+        def multiply(c):
+            lo, hi = CHUNKS[c]
             acc = psum.tile([NQ, hi - lo], F32, name=f"acc{c}")
             nc.tensor.matmul_mx(
                 out=acc[:],
@@ -86,19 +95,25 @@ def tile_attend_sddmm_kernel(tc, qT, kT, offs, out):
                 start=True,
                 stop=True,
             )
-            nc.scalar.copy(results[c][:], acc[:])
+            nc.scalar.copy(result[:, lo:hi], acc[:])
 
-        def scatter(c):
-            lo, hi = CHUNKS[c]
-            nc.vector.tensor_copy(window[:].indirect(offsets[:, lo // 16 : hi // 16]), results[c][:])
+        def scatter(lo, hi):
+            nc.vector.tensor_copy(window[:].indirect(offsets[:, lo // 16 : hi // 16]), result[:, lo:hi])
 
-        gather(0)
-        gather(1)
+        on_vector(3, 0, 128)
+        on_vector(3, 128, 256)
+        nc.vector.tensor_copy(q_grouped[:], q_raw[:].rearrange("p j q -> p q j"))
+        nc.vector.quantize_mx(
+            out=q_codes[:].bitcast(FP8X4),
+            scales=q_scales[:],
+            in_=q_grouped[:].rearrange("p q j -> p (q j)"),
+        )
+        quantise(0)
         multiply(0)
-        gather(2)
+        quantise(1)
         multiply(1)
-        scatter(0)
+        quantise(2)
         multiply(2)
-        scatter(1)
-        scatter(2)
+        scatter(0, 128)
+        scatter(128, 512)
         nc.sync.dma_start(out[0], window[:])

@@ -31,8 +31,11 @@ def tile_attend_sddmm_kernel(tc, qT, kT, offs, out):
         planes = [keep.tile([P, T], F32, name=f"plane{j}") for j in range(PACK)]
         q_raw = keep.tile([P, PACK, NQ], F32, name="q_raw")
 
+        first = slice(0, T // 2)
+        second = slice(T // 2, T)
+        nc.sync.dma_start(planes[0][:, first], k_rows[0][:, first])
+        nc.sync.dma_start(planes[0][:, second], k_rows[0][:, second])
         nc.sync.dma_start(offsets[:], offs)
-        nc.sync.dma_start(planes[0][:], k_rows[0])
         nc.sync.dma_start(planes[1][:], k_rows[1])
         nc.sync.dma_start(planes[2][:], k_rows[2])
         nc.sync.dma_start(planes[3][:], k_rows[3])
@@ -58,14 +61,25 @@ def tile_attend_sddmm_kernel(tc, qT, kT, offs, out):
         def on_scalar(j, lo, hi):
             nc.scalar.activation(keys[:, lo:hi, j], rounded[j][:].indirect(offsets[:, lo // 16 : hi // 16]), COPY)
 
-        for j in (0, 1):
-            nc.vector.tensor_copy(rounded[j][:], planes[j][:])
-            on_scalar(j, 0, 256)
-            on_vector(j, 256, 512)
-        nc.scalar.activation(rounded[2][:], planes[2][:], COPY)
+        def cast_on_vector(j, cols):
+            nc.vector.tensor_copy(rounded[j][:, cols], planes[j][:, cols])
+
+        def cast_on_scalar(j, cols):
+            nc.scalar.activation(rounded[j][:, cols], planes[j][:, cols], COPY)
+
+        cast_on_vector(0, first)
+        cast_on_vector(0, second)
+        on_scalar(0, 0, 256)
+        on_vector(0, 256, 512)
+        cast_on_vector(1, first)
+        cast_on_scalar(1, second)
+        on_scalar(1, 0, 256)
+        on_vector(1, 256, 512)
+        cast_on_vector(2, second)
+        cast_on_scalar(2, first)
         on_scalar(2, 256, 512)
         on_vector(2, 0, 256)
-        nc.vector.tensor_copy(rounded[3][:], planes[3][:])
+        cast_on_vector(3, slice(0, T))
         on_scalar(3, 256, 512)
 
         codes = []

@@ -2,20 +2,26 @@ from contextlib import ExitStack
 
 import concourse.mybir as mybir
 
-N, T, D, NQ = 512, 1024, 512, 128
+SLOTS, TOKENS, FEATURES, QUERIES = 512, 1024, 512, 128
 P = 128
 PACK = 4
-FLOPS = 2 * NQ * D * N
+CHUNK = 128
+OFFSETS_A_COLUMN = 16
+
+EARLY_SPLIT = 256
+LATE_SPLIT = 128
+LAST_CUT = 384
+SCATTER_SPLIT = 128
+
+FLOPS = 2 * QUERIES * FEATURES * SLOTS
 
 F32 = mybir.dt.float32
 BF16 = mybir.dt.bfloat16
 U32 = mybir.dt.uint32
 U16 = mybir.dt.uint16
 U8 = mybir.dt.uint8
-COPY = mybir.ActivationFunctionType.Copy
 FP8X4 = mybir.dt.float8_e4m3fn_x4
-
-CHUNKS = ((0, 128), (128, 256), (256, 512))
+COPY = mybir.ActivationFunctionType.Copy
 
 
 def tile_attend_sddmm_kernel(tc, qT, kT, offs, out):
@@ -27,107 +33,102 @@ def tile_attend_sddmm_kernel(tc, qT, kT, offs, out):
         keep = ctx.enter_context(tc.tile_pool(name="keep", bufs=1))
         psum = ctx.enter_context(tc.psum_pool(name="psum", bufs=1))
 
-        offsets = keep.tile([P, N // 16], U16, name="offsets")
-        planes = [keep.tile([P, T], F32, name=f"plane{j}") for j in range(PACK)]
-        q_raw = keep.tile([P, PACK, NQ], F32, name="q_raw")
+        offsets = keep.tile([P, SLOTS // OFFSETS_A_COLUMN], U16, name="offsets")
+        planes = [keep.tile([P, TOKENS], F32, name=f"plane{j}") for j in range(PACK)]
+        q_raw = keep.tile([P, PACK, QUERIES], F32, name="q_raw")
 
-        first = slice(0, T // 2)
-        second = slice(T // 2, T)
-        nc.sync.dma_start(planes[0][:, first], k_rows[0][:, first])
-        nc.sync.dma_start(planes[0][:, second], k_rows[0][:, second])
+        whole = slice(0, TOKENS)
+        first_half = slice(0, TOKENS // 2)
+        second_half = slice(TOKENS // 2, TOKENS)
+        nc.sync.dma_start(planes[0][:, first_half], k_rows[0][:, first_half])
+        nc.sync.dma_start(planes[0][:, second_half], k_rows[0][:, second_half])
         nc.sync.dma_start(offsets[:], offs)
-        nc.sync.dma_start(planes[1][:], k_rows[1])
-        nc.sync.dma_start(planes[2][:], k_rows[2])
-        nc.sync.dma_start(planes[3][:], k_rows[3])
+        for j in range(1, PACK):
+            nc.sync.dma_start(planes[j][:], k_rows[j])
         nc.sync.dma_start(q_raw[:], q_rows)
 
-        window = keep.tile([P, T], F32, name="window")
+        window = keep.tile([P, TOKENS], F32, name="window")
         nc.vector.memset(window[:], 0.0)
 
-        warm = keep.tile([P, 8], F32, name="warm")
-        warmed = keep.tile([P, 8], F32, name="warmed")
-        nc.vector.memset(warm[:], 0.0)
-        nc.scalar.activation(warmed[:], warm[:], COPY)
+        warm_in = keep.tile([P, 8], F32, name="warm_in")
+        warm_out = keep.tile([P, 8], F32, name="warm_out")
+        nc.vector.memset(warm_in[:], 0.0)
+        nc.scalar.activation(warm_out[:], warm_in[:], COPY)
 
-        rounded = [keep.tile([P, T], BF16, name=f"rounded{j}") for j in range(PACK)]
-        keys = keep.tile([P, N, PACK], BF16, align_bytes=64, name="keys")
-        q_grouped = keep.tile([P, NQ, PACK], BF16, align_bytes=64, name="q_grouped")
-        q_codes = keep.tile([P, NQ], U32, align_bytes=64, name="q_codes")
-        q_scales = keep.tile([P, NQ], U8, align_bytes=64, name="q_scales")
+        rounded = [keep.tile([P, TOKENS], BF16, name=f"rounded{j}") for j in range(PACK)]
+        keys = keep.tile([P, SLOTS, PACK], BF16, align_bytes=64, name="keys")
+        q_grouped = keep.tile([P, QUERIES, PACK], BF16, align_bytes=64, tag="stage", name="q_grouped")
+        q_codes = keep.tile([P, QUERIES], U32, align_bytes=64, name="q_codes")
+        q_scales = keep.tile([P, QUERIES], U8, align_bytes=64, name="q_scales")
 
-        def on_vector(j, lo, hi):
-            nc.vector.tensor_copy(keys[:, lo:hi, j], planes[j][:].indirect(offsets[:, lo // 16 : hi // 16]))
+        def listed(tile, lo, hi):
+            return tile[:].indirect(offsets[:, lo // OFFSETS_A_COLUMN : hi // OFFSETS_A_COLUMN])
 
-        def on_scalar(j, lo, hi):
-            nc.scalar.activation(keys[:, lo:hi, j], rounded[j][:].indirect(offsets[:, lo // 16 : hi // 16]), COPY)
+        def gather_on_vector(j, lo, hi):
+            nc.vector.tensor_copy(keys[:, lo:hi, j], listed(planes[j], lo, hi))
 
-        def cast_on_vector(j, cols):
-            nc.vector.tensor_copy(rounded[j][:, cols], planes[j][:, cols])
+        def gather_on_scalar(j, lo, hi):
+            nc.scalar.activation(keys[:, lo:hi, j], listed(rounded[j], lo, hi), COPY)
 
-        def cast_on_scalar(j, cols):
-            nc.scalar.activation(rounded[j][:, cols], planes[j][:, cols], COPY)
+        def cast_on_vector(j, columns):
+            nc.vector.tensor_copy(rounded[j][:, columns], planes[j][:, columns])
 
-        cast_on_vector(0, first)
-        cast_on_vector(0, second)
-        on_scalar(0, 0, 256)
-        on_vector(0, 256, 512)
-        cast_on_vector(1, first)
-        cast_on_scalar(1, second)
-        on_scalar(1, 0, 256)
-        on_vector(1, 256, 512)
-        cast_on_vector(2, second)
-        cast_on_scalar(2, first)
-        on_scalar(2, 256, 512)
-        on_vector(2, 0, 256)
-        cast_on_vector(3, slice(0, T))
-        on_scalar(3, 256, 512)
+        def cast_on_scalar(j, columns):
+            nc.scalar.activation(rounded[j][:, columns], planes[j][:, columns], COPY)
 
-        codes = []
-        scales = []
-        result = keep.tile([NQ, N], F32, name="result")
-        for c, (lo, hi) in enumerate(CHUNKS):
-            codes.append(keep.tile([P, hi - lo], U32, align_bytes=64, name=f"codes{c}"))
-            scales.append(keep.tile([P, hi - lo], U8, align_bytes=64, name=f"scales{c}"))
+        cast_on_vector(0, first_half)
+        cast_on_vector(0, second_half)
+        gather_on_scalar(0, 0, EARLY_SPLIT)
+        gather_on_vector(0, EARLY_SPLIT, SLOTS)
+        cast_on_vector(1, first_half)
+        cast_on_scalar(1, second_half)
+        gather_on_scalar(1, 0, EARLY_SPLIT)
+        gather_on_vector(1, EARLY_SPLIT, SLOTS)
+        cast_on_vector(2, whole)
+        gather_on_scalar(2, LATE_SPLIT, SLOTS)
+        gather_on_vector(2, 0, LATE_SPLIT)
+        cast_on_vector(3, whole)
+        gather_on_scalar(3, LATE_SPLIT, LAST_CUT)
+        gather_on_scalar(3, LAST_CUT, SLOTS)
 
-        def quantise(c):
-            lo, hi = CHUNKS[c]
-            nc.vector.quantize_mx(
-                out=codes[c][:].bitcast(FP8X4),
-                scales=scales[c][:],
-                in_=keys[:, lo:hi, :].rearrange("p n j -> p (n j)"),
-            )
+        result = keep.tile([QUERIES, SLOTS], F32, name="result")
+        first_codes = keep.tile([P, CHUNK], U32, align_bytes=64, name="first_codes")
+        scales = [keep.tile([P, CHUNK], U8, align_bytes=64, name=f"scales{c}") for c in range(SLOTS // CHUNK)]
 
-        def multiply(c):
-            lo, hi = CHUNKS[c]
-            acc = psum.tile([NQ, hi - lo], F32, name=f"acc{c}")
-            nc.tensor.matmul_mx(
-                out=acc[:],
-                lhsT=q_codes[:].bitcast(FP8X4),
-                lhsT_scale=q_scales[:],
-                rhs=codes[c][:].bitcast(FP8X4),
-                rhs_scale=scales[c][:],
-                start=True,
-                stop=True,
-            )
-            nc.scalar.copy(result[:, lo:hi], acc[:])
-
-        def scatter(lo, hi):
-            nc.vector.tensor_copy(window[:].indirect(offsets[:, lo // 16 : hi // 16]), result[:, lo:hi])
-
-        on_vector(3, 0, 128)
-        on_vector(3, 128, 256)
+        gather_on_vector(3, 0, LATE_SPLIT)
         nc.vector.tensor_copy(q_grouped[:], q_raw[:].rearrange("p j q -> p q j"))
         nc.vector.quantize_mx(
             out=q_codes[:].bitcast(FP8X4),
             scales=q_scales[:],
             in_=q_grouped[:].rearrange("p q j -> p (q j)"),
         )
-        quantise(0)
-        multiply(0)
-        quantise(1)
-        multiply(1)
-        quantise(2)
-        multiply(2)
-        scatter(0, 128)
-        scatter(128, 512)
+
+        late_codes = keep.tile([P, SLOTS - CHUNK], U32, align_bytes=64, tag="stage", name="late_codes")
+
+        def codes_of(c):
+            if c == 0:
+                return first_codes[:]
+            return late_codes[:, (c - 1) * CHUNK : c * CHUNK]
+
+        for c in range(SLOTS // CHUNK):
+            slots = slice(c * CHUNK, (c + 1) * CHUNK)
+            nc.vector.quantize_mx(
+                out=codes_of(c).bitcast(FP8X4),
+                scales=scales[c][:],
+                in_=keys[:, slots, :].rearrange("p n j -> p (n j)"),
+            )
+            acc = psum.tile([QUERIES, CHUNK], F32, name=f"acc{c}")
+            nc.tensor.matmul_mx(
+                out=acc[:],
+                lhsT=q_codes[:].bitcast(FP8X4),
+                lhsT_scale=q_scales[:],
+                rhs=codes_of(c).bitcast(FP8X4),
+                rhs_scale=scales[c][:],
+                start=True,
+                stop=True,
+            )
+            nc.scalar.copy(result[:, slots], acc[:])
+
+        for lo, hi in ((0, SCATTER_SPLIT), (SCATTER_SPLIT, SLOTS)):
+            nc.vector.tensor_copy(listed(window, lo, hi), result[:, lo:hi])
         nc.sync.dma_start(out[0], window[:])

from contextlib import ExitStack

import concourse.mybir as mybir

SLOTS, TOKENS, FEATURES, QUERIES = 512, 1024, 512, 128
P = 128
PACK = 4
CHUNK = 128
OFFSETS_A_COLUMN = 16

EARLY_SPLIT = 256
LATE_SPLIT = 128
LAST_CUT = 384
SCATTER_SPLIT = 128

FLOPS = 2 * QUERIES * FEATURES * SLOTS

F32 = mybir.dt.float32
BF16 = mybir.dt.bfloat16
U32 = mybir.dt.uint32
U16 = mybir.dt.uint16
U8 = mybir.dt.uint8
FP8X4 = mybir.dt.float8_e4m3fn_x4
COPY = mybir.ActivationFunctionType.Copy


def tile_attend_sddmm_kernel(tc, qT, kT, offs, out):
    nc = tc.nc
    k_rows = kT.rearrange("(p j) t -> j p t", j=PACK)
    q_rows = qT[0].rearrange("(p j) q -> p j q", j=PACK)

    with ExitStack() as ctx:
        keep = ctx.enter_context(tc.tile_pool(name="keep", bufs=1))
        psum = ctx.enter_context(tc.psum_pool(name="psum", bufs=1))

        offsets = keep.tile([P, SLOTS // OFFSETS_A_COLUMN], U16, name="offsets")
        planes = [keep.tile([P, TOKENS], F32, name=f"plane{j}") for j in range(PACK)]
        q_raw = keep.tile([P, PACK, QUERIES], F32, name="q_raw")

        whole = slice(0, TOKENS)
        first_half = slice(0, TOKENS // 2)
        second_half = slice(TOKENS // 2, TOKENS)
        nc.sync.dma_start(planes[0][:, first_half], k_rows[0][:, first_half])
        nc.sync.dma_start(planes[0][:, second_half], k_rows[0][:, second_half])
        nc.sync.dma_start(offsets[:], offs)
        for j in range(1, PACK):
            nc.sync.dma_start(planes[j][:], k_rows[j])
        nc.sync.dma_start(q_raw[:], q_rows)

        window = keep.tile([P, TOKENS], F32, name="window")
        nc.vector.memset(window[:], 0.0)

        warm_in = keep.tile([P, 8], F32, name="warm_in")
        warm_out = keep.tile([P, 8], F32, name="warm_out")
        nc.vector.memset(warm_in[:], 0.0)
        nc.scalar.activation(warm_out[:], warm_in[:], COPY)

        rounded = [keep.tile([P, TOKENS], BF16, name=f"rounded{j}") for j in range(PACK)]
        keys = keep.tile([P, SLOTS, PACK], BF16, align_bytes=64, name="keys")
        q_grouped = keep.tile([P, QUERIES, PACK], BF16, align_bytes=64, tag="stage", name="q_grouped")
        q_codes = keep.tile([P, QUERIES], U32, align_bytes=64, name="q_codes")
        q_scales = keep.tile([P, QUERIES], U8, align_bytes=64, name="q_scales")

        def listed(tile, lo, hi):
            return tile[:].indirect(offsets[:, lo // OFFSETS_A_COLUMN : hi // OFFSETS_A_COLUMN])

        def gather_on_vector(j, lo, hi):
            nc.vector.tensor_copy(keys[:, lo:hi, j], listed(planes[j], lo, hi))

        def gather_on_scalar(j, lo, hi):
            nc.scalar.activation(keys[:, lo:hi, j], listed(rounded[j], lo, hi), COPY)

        def cast_on_vector(j, columns):
            nc.vector.tensor_copy(rounded[j][:, columns], planes[j][:, columns])

        def cast_on_scalar(j, columns):
            nc.scalar.activation(rounded[j][:, columns], planes[j][:, columns], COPY)

        cast_on_vector(0, first_half)
        cast_on_vector(0, second_half)
        gather_on_scalar(0, 0, EARLY_SPLIT)
        gather_on_vector(0, EARLY_SPLIT, SLOTS)
        cast_on_vector(1, first_half)
        cast_on_scalar(1, second_half)
        gather_on_scalar(1, 0, EARLY_SPLIT)
        gather_on_vector(1, EARLY_SPLIT, SLOTS)
        cast_on_vector(2, whole)
        gather_on_scalar(2, LATE_SPLIT, SLOTS)
        gather_on_vector(2, 0, LATE_SPLIT)
        cast_on_vector(3, whole)
        gather_on_scalar(3, LATE_SPLIT, LAST_CUT)
        gather_on_scalar(3, LAST_CUT, SLOTS)

        result = keep.tile([QUERIES, SLOTS], F32, name="result")
        first_codes = keep.tile([P, CHUNK], U32, align_bytes=64, name="first_codes")
        scales = [keep.tile([P, CHUNK], U8, align_bytes=64, name=f"scales{c}") for c in range(SLOTS // CHUNK)]

        gather_on_vector(3, 0, LATE_SPLIT)
        nc.vector.tensor_copy(q_grouped[:], q_raw[:].rearrange("p j q -> p q j"))
        nc.vector.quantize_mx(
            out=q_codes[:].bitcast(FP8X4),
            scales=q_scales[:],
            in_=q_grouped[:].rearrange("p q j -> p (q j)"),
        )

        late_codes = keep.tile([P, SLOTS - CHUNK], U32, align_bytes=64, tag="stage", name="late_codes")

        def codes_of(c):
            if c == 0:
                return first_codes[:]
            return late_codes[:, (c - 1) * CHUNK : c * CHUNK]

        for c in range(SLOTS // CHUNK):
            slots = slice(c * CHUNK, (c + 1) * CHUNK)
            nc.vector.quantize_mx(
                out=codes_of(c).bitcast(FP8X4),
                scales=scales[c][:],
                in_=keys[:, slots, :].rearrange("p n j -> p (n j)"),
            )
            acc = psum.tile([QUERIES, CHUNK], F32, name=f"acc{c}")
            nc.tensor.matmul_mx(
                out=acc[:],
                lhsT=q_codes[:].bitcast(FP8X4),
                lhsT_scale=q_scales[:],
                rhs=codes_of(c).bitcast(FP8X4),
                rhs_scale=scales[c][:],
                start=True,
                stop=True,
            )
            nc.scalar.copy(result[:, slots], acc[:])

        for lo, hi in ((0, SCATTER_SPLIT), (SCATTER_SPLIT, SLOTS)):
            nc.vector.tensor_copy(listed(window, lo, hi), result[:, lo:hi])
        nc.sync.dma_start(out[0], window[:])
